import numpy as np
import ml_dtypes


def mxq(x, axis, fmt="e4m3"):
    dtype, down = {"e4m3": (ml_dtypes.float8_e4m3fn, 7), "e5m2": (ml_dtypes.float8_e5m2, 14)}[fmt]
    v = np.moveaxis(np.asarray(x, np.float32).astype(ml_dtypes.bfloat16).astype(np.float64), axis, -1)
    blocks = v.reshape(v.shape[:-1] + (-1, 32))
    amax = np.abs(blocks).max(-1, keepdims=True)
    byte = np.maximum(np.where(amax > 0, np.frexp(amax)[1] - 1 + 127, 0) - down, 1)
    scale = np.exp2(byte - 127.0)
    codes = (blocks / scale).astype(np.float32).astype(dtype).astype(np.float64)
    return np.moveaxis((codes * scale).reshape(v.shape), -1, axis)


WIDE = False


def mx_kscale(k):
    if not WIDE:
        return np.ones(k)
    levels = np.array([10, -10, 5, -5, 0])
    if k % 512:
        return np.exp2(np.random.permutation(np.resize(levels, k // 32))).repeat(32)
    a = np.empty((k // 512, 16))
    for p in range(k // 512):
        a[p, :8] = np.random.permutation(np.resize(levels, 8))
        for g in range(8):
            far = levels[np.abs(levels - a[p, g]) >= 10]
            a[p, g + 8] = far[np.random.randint(len(far))]
    return np.exp2(a.ravel()).repeat(32)


def f64(x):
    return np.asarray(x).astype(np.float64)


def striped(idx):
    return np.tile(idx.reshape(-1, 16).T, (8, 1)).astype(np.uint16)


def unstriped(offs):
    return offs[:16].T.reshape(-1).astype(np.int64)


K, T, E, C, N = 2048, 1024, 8, 128, 128


def by_expert(wq, xq):
    return np.concatenate([wq[e].T @ xq[:, e * C:(e + 1) * C] for e in range(E)], axis=1)


def setup_inputs():
    n = np.random.standard_normal
    s = mx_kscale(K)[:, None]
    return {
        "xT": (n((K, T)) * s).astype(np.float32),
        "w": (n((E, K, N)) / np.sqrt(K) / s[None]).astype(np.float32),
        "offs": striped(np.random.permutation(T)[:E * C]),
    }


def reference(xT, w, offs):
    idx = unstriped(offs)
    xq = mxq(f64(xT)[:, idx], 0, "e4m3")
    y = by_expert(mxq(f64(w), 1, "e4m3"), xq)
    out = np.zeros((N, T))
    out[:, idx] = y
    return out

@@ -1,0 +1,178 @@
+from contextlib import ExitStack
+
+import concourse.mybir as mybir
+
+K, T, E, C, N = 2048, 1024, 8, 128, 128
+FLOPS = 2 * K * N * E * C
+
+F32 = mybir.dt.float32
+BF16 = mybir.dt.bfloat16
+U32 = mybir.dt.uint32
+I32 = mybir.dt.int32
+U16 = mybir.dt.uint16
+U8 = mybir.dt.uint8
+FP8X4 = mybir.dt.float8_e4m3fn_x4
+
+P = 128
+PASSES = K // (4 * P)
+CHUNKS = 2 * PASSES
+HALF = T // 2
+BANK = 4
+HEAD_CUTS = (4, 2)
+
+
+def tile_routed_moe_kernel(tc, xT, w, offs, out):
+    nc = tc.nc
+    with ExitStack() as ctx:
+        keep = ctx.enter_context(tc.tile_pool(name="keep", bufs=1))
+        raw_pool = ctx.enter_context(tc.tile_pool(name="raw_pool", bufs=7))
+        head_pool = ctx.enter_context(tc.tile_pool(name="head_pool", bufs=1))
+        last_pool = ctx.enter_context(tc.tile_pool(name="last_pool", bufs=1))
+        slot_pool = ctx.enter_context(tc.tile_pool(name="slot_pool", bufs=2))
+        weight_pool = ctx.enter_context(tc.tile_pool(name="weight_pool", bufs=E // 2))
+        psum = ctx.enter_context(tc.psum_pool(name="psum", bufs=E // BANK))
+
+        offsets = keep.tile([P, T // 16], U16, name="offsets")
+        nc.sync.dma_start(offsets[:], offs)
+
+        pairs = keep.tile([P, CHUNKS, T, 2], BF16, name="pairs", align_bytes=64)
+        pair_words = pairs[:].rearrange("p r n e -> p (r n e)").bitcast(U32)
+        x_codes = keep.tile([P, PASSES, T], U32, name="x_codes", align_bytes=64)
+        x_scales = keep.tile([P, PASSES, T], U8, name="x_scales", align_bytes=64)
+        w_codes = keep.tile([P, E, PASSES * N], U32, name="w_codes", align_bytes=64)
+        w_scales = keep.tile([P, E, PASSES * N], U8, name="w_scales", align_bytes=64)
+        out_sb = keep.tile([P, T], F32, name="out_sb")
+
+        x_view = xT.rearrange("(g p u e) n -> g u p e n", g=PASSES, p=P, u=2, e=2)
+        x_raw = []
+        for i in range(CHUNKS):
+            src = x_view[i // 2, i % 2]
+            if i < 2:
+                pieces = []
+                cuts = HEAD_CUTS[i]
+                for h in range(cuts):
+                    part = head_pool.tile([P, 2, T // cuts], F32, name="part%d_%d" % (i, h))
+                    nc.sync.dma_start(part[:], src[:, :, h * (T // cuts) : (h + 1) * (T // cuts)])
+                    pieces.append(part)
+            else:
+                raw = raw_pool.tile([P, 2, T], F32, name="raw", tag="raw")
+                nc.sync.dma_start(raw[:], src)
+                pieces = [raw]
+            x_raw.append(pieces)
+        w_raw = []
+        for e in range(E):
+            src = w[e].rearrange("(g p t) n -> p g (t n)", p=P, t=4)
+            if e < E - 1:
+                raw = raw_pool.tile([P, PASSES, 4 * N], F32, name="raw", tag="raw")
+                nc.sync.dma_start(raw[:], src)
+                w_raw.append([raw])
+            else:
+                early = head_pool.tile([P, PASSES // 2, 4 * N], F32, name="early")
+                nc.sync.dma_start(early[:], src[:, 0 : PASSES // 2, :])
+                late = last_pool.tile([P, PASSES // 2, 4 * N], F32, name="last", tag="last")
+                nc.sync.dma_start(late[:], src[:, PASSES // 2 : PASSES, :])
+                w_raw.append([early, late])
+
+        def cast_x(i):
+            region = pairs[:, CHUNKS - 1 - i]
+            width = T // len(x_raw[i])
+            for h, piece in enumerate(x_raw[i]):
+                dst = region[:, h * width : (h + 1) * width, :]
+                src = piece[:].rearrange("p e n -> p n e")
+                if i == 0:
+                    nc.vector.tensor_copy(out=dst, in_=src)
+                else:
+                    nc.scalar.copy(out=dst, in_=src)
+
+        gathered = {}
+        grouped = {}
+
+        def gather_x(i):
+            g, u = i // 2, i % 2
+            r = CHUNKS - 1 - i
+            if u == 0:
+                planes = slot_pool.tile([P, 2, T], U32, name="planes", align_bytes=64)
+                gathered[g] = planes
+            dst = gathered[g][:, u, :]
+            if i == 0:
+                for s0 in range(0, T, HALF):
+                    nc.vector.tensor_copy(
+                        out=dst[:, s0 : s0 + HALF],
+                        in_=pair_words[:, r * T : (r + 1) * T].indirect(offsets[:, s0 // 16 : (s0 + HALF) // 16]),
+                    )
+            else:
+                nc.vector.tensor_copy(out=dst, in_=pair_words[:, r * T : (r + 2) * T].indirect(offsets[:]))
+
+        def interleave_x(g):
+            quads = slot_pool.tile([P, T * 4], BF16, name="quads", align_bytes=64)
+            grouped[g] = quads
+            nc.vector.tensor_copy(
+                out=quads[:].bitcast(I32).rearrange("p (s u) -> p s u", u=2),
+                in_=gathered[g][:].bitcast(I32).rearrange("p u s -> p s u"),
+            )
+
+        def quantize_x(g):
+            nc.vector.quantize_mx(out=x_codes[:, g, :].bitcast(FP8X4), scales=x_scales[:, g, :], in_=grouped[g][:])
+
+        for i in range(CHUNKS):
+            cast_x(i)
+        for i in range(CHUNKS):
+            gather_x(i)
+            if i >= 2 and i % 2 == 0:
+                interleave_x(i // 2 - 1)
+            if i >= 3 and i % 2 == 1:
+                quantize_x(i // 2 - 1)
+        interleave_x(PASSES - 1)
+
+        w_grouped = []
+        for d in range(E // 2):
+            duo = weight_pool.tile([P, 2, PASSES, N, 4], BF16, name="duo", align_bytes=64)
+            w_grouped.append(duo)
+            for j in range(2):
+                pieces = w_raw[2 * d + j]
+                span = PASSES // len(pieces)
+                for h, piece in enumerate(pieces):
+                    nc.scalar.copy(
+                        out=duo[:, j, h * span : (h + 1) * span].rearrange("p g (c i) t -> p g c t i", i=4),
+                        in_=piece[:].rearrange("p g (t c i) -> p g c t i", t=4, i=4),
+                    )
+
+        sums = last_pool.tile([P, T], F32, name="last", tag="last")
+        for d in range(E // 2):
+            if d < E // 2 - 1:
+                nc.vector.quantize_mx(
+                    out=w_codes[:, 2 * d : 2 * d + 2, :].rearrange("p e c -> p (e c)").bitcast(FP8X4),
+                    scales=w_scales[:, 2 * d : 2 * d + 2, :].rearrange("p e c -> p (e c)"),
+                    in_=w_grouped[d][:].rearrange("p j g n t -> p (j g n t)"),
+                )
+            else:
+                for j in range(2):
+                    nc.vector.quantize_mx(
+                        out=w_codes[:, 2 * d + j, :].bitcast(FP8X4),
+                        scales=w_scales[:, 2 * d + j, :],
+                        in_=w_grouped[d][:, j].rearrange("p g n t -> p (g n t)"),
+                    )
+            if d == 0:
+                quantize_x(PASSES - 1)
+            if d % 2 == 0:
+                acc = psum.tile([P, BANK * C], F32, name="acc")
+            for e in (2 * d, 2 * d + 1):
+                for g in range(PASSES):
+                    nc.tensor.matmul_mx(
+                        out=acc[:, (e % BANK) * C : (e % BANK + 1) * C],
+                        lhsT=w_codes[:, e, g * N : (g + 1) * N].bitcast(FP8X4),
+                        lhsT_scale=w_scales[:, e, g * N : (g + 1) * N],
+                        rhs=x_codes[:, g, e * C : (e + 1) * C].bitcast(FP8X4),
+                        rhs_scale=x_scales[:, g, e * C : (e + 1) * C],
+                        start=(g == 0),
+                        stop=(g == PASSES - 1),
+                    )
+            if d % 2 == 1:
+                s0 = (d // 2) * BANK * C
+                nc.scalar.copy(out=sums[:, s0 : s0 + BANK * C], in_=acc[:])
+        for s0 in range(0, T, BANK * C):
+            nc.vector.tensor_copy(
+                out=out_sb[:].indirect(offsets[:, s0 // 16 : (s0 + BANK * C) // 16]),
+                in_=sums[:, s0 : s0 + BANK * C],
+            )
+        nc.sync.dma_start(out, out_sb[:])

@@ -19,6 +19,9 @@ CHUNKS = 2 * PASSES
 HALF = T // 2
 BANK = 4
 HEAD_CUTS = (4, 2)
+V_SLOTS = 256
+MULT = mybir.AluOpType.mult
+ADD = mybir.AluOpType.add
 
 
 def tile_routed_moe_kernel(tc, xT, w, offs, out):
@@ -103,12 +106,25 @@ def tile_routed_moe_kernel(tc, xT, w, offs, out):
             else:
                 nc.vector.tensor_copy(out=dst, in_=pair_words[:, r * T : (r + 2) * T].indirect(offsets[:]))
 
-        def interleave_x(g):
+        def open_quads(g):
             quads = slot_pool.tile([P, T * 4], BF16, name="quads", align_bytes=64)
             grouped[g] = quads
+
+        def interleave_pool(g, s0):
+            src = gathered[g][:].rearrange("p u s -> p (u s)").bitcast(BF16)
+            nc.gpsimd.tensor_scalar(
+                out=grouped[g][:].rearrange("p (s u e) -> p s u e", u=2, e=2)[:, s0:T],
+                in0=src.rearrange("p (u s e) -> p s u e", u=2, e=2)[:, s0:T],
+                scalar1=1.0,
+                scalar2=0.0,
+                op0=MULT,
+                op1=ADD,
+            )
+
+        def interleave_vector(g, s1):
             nc.vector.tensor_copy(
-                out=quads[:].bitcast(I32).rearrange("p (s u) -> p s u", u=2),
-                in_=gathered[g][:].bitcast(I32).rearrange("p u s -> p s u"),
+                out=grouped[g][:].bitcast(I32).rearrange("p (s u) -> p s u", u=2)[:, 0:s1],
+                in_=gathered[g][:].bitcast(I32).rearrange("p u s -> p s u")[:, 0:s1],
             )
 
         def quantize_x(g):
@@ -116,13 +132,19 @@ def tile_routed_moe_kernel(tc, xT, w, offs, out):
 
         for i in range(CHUNKS):
             cast_x(i)
-        for i in range(CHUNKS):
-            gather_x(i)
-            if i >= 2 and i % 2 == 0:
-                interleave_x(i // 2 - 1)
-            if i >= 3 and i % 2 == 1:
-                quantize_x(i // 2 - 1)
-        interleave_x(PASSES - 1)
+        for g in range(PASSES):
+            if g >= 1:
+                open_quads(g - 1)
+                interleave_pool(g - 1, V_SLOTS)
+            gather_x(2 * g)
+            gather_x(2 * g + 1)
+            if g >= 1:
+                interleave_vector(g - 1, V_SLOTS)
+            if g >= 2:
+                quantize_x(g - 2)
+        open_quads(PASSES - 1)
+        interleave_vector(PASSES - 1, T)
+        quantize_x(PASSES - 2)
 
         w_grouped = []
         for d in range(E // 2):

@@ -19,9 +19,6 @@ CHUNKS = 2 * PASSES
 HALF = T // 2
 BANK = 4
 HEAD_CUTS = (4, 2)
-V_SLOTS = 256
-MULT = mybir.AluOpType.mult
-ADD = mybir.AluOpType.add
 
 
 def tile_routed_moe_kernel(tc, xT, w, offs, out):
@@ -111,20 +108,9 @@ def tile_routed_moe_kernel(tc, xT, w, offs, out):
             grouped[g] = quads
 
         def interleave_pool(g, s0):
-            src = gathered[g][:].rearrange("p u s -> p (u s)").bitcast(BF16)
-            nc.gpsimd.tensor_scalar(
-                out=grouped[g][:].rearrange("p (s u e) -> p s u e", u=2, e=2)[:, s0:T],
-                in0=src.rearrange("p (u s e) -> p s u e", u=2, e=2)[:, s0:T],
-                scalar1=1.0,
-                scalar2=0.0,
-                op0=MULT,
-                op1=ADD,
-            )
-
-        def interleave_vector(g, s1):
-            nc.vector.tensor_copy(
-                out=grouped[g][:].bitcast(I32).rearrange("p (s u) -> p s u", u=2)[:, 0:s1],
-                in_=gathered[g][:].bitcast(I32).rearrange("p u s -> p s u")[:, 0:s1],
+            nc.gpsimd.tensor_copy(
+                out=grouped[g][:].bitcast(I32).rearrange("p (s u) -> p s u", u=2)[:, s0:T],
+                in_=gathered[g][:].bitcast(I32).rearrange("p u s -> p s u")[:, s0:T],
             )
 
         def quantize_x(g):
@@ -133,18 +119,12 @@ def tile_routed_moe_kernel(tc, xT, w, offs, out):
         for i in range(CHUNKS):
             cast_x(i)
         for g in range(PASSES):
-            if g >= 1:
-                open_quads(g - 1)
-                interleave_pool(g - 1, V_SLOTS)
             gather_x(2 * g)
             gather_x(2 * g + 1)
+            open_quads(g)
+            interleave_pool(g, 0)
             if g >= 1:
-                interleave_vector(g - 1, V_SLOTS)
-            if g >= 2:
-                quantize_x(g - 2)
-        open_quads(PASSES - 1)
-        interleave_vector(PASSES - 1, T)
-        quantize_x(PASSES - 2)
+                quantize_x(g - 1)
 
         w_grouped = []
         for d in range(E // 2):

@@ -107,10 +107,16 @@ def tile_routed_moe_kernel(tc, xT, w, offs, out):
             quads = slot_pool.tile([P, T * 4], BF16, name="quads", align_bytes=64)
             grouped[g] = quads
 
-        def interleave_pool(g, s0):
+        def interleave_pool(g):
             nc.gpsimd.tensor_copy(
-                out=grouped[g][:].bitcast(I32).rearrange("p (s u) -> p s u", u=2)[:, s0:T],
-                in_=gathered[g][:].bitcast(I32).rearrange("p u s -> p s u")[:, s0:T],
+                out=grouped[g][:].bitcast(I32).rearrange("p (s u) -> p s u", u=2),
+                in_=gathered[g][:].bitcast(I32).rearrange("p u s -> p s u"),
+            )
+
+        def interleave_vector(g):
+            nc.vector.tensor_copy(
+                out=grouped[g][:].bitcast(I32).rearrange("p (s u) -> p s u", u=2),
+                in_=gathered[g][:].bitcast(I32).rearrange("p u s -> p s u"),
             )
 
         def quantize_x(g):
@@ -122,7 +128,10 @@ def tile_routed_moe_kernel(tc, xT, w, offs, out):
             gather_x(2 * g)
             gather_x(2 * g + 1)
             open_quads(g)
-            interleave_pool(g, 0)
+            if g < PASSES - 1:
+                interleave_pool(g)
+            else:
+                interleave_vector(g)
             if g >= 1:
                 quantize_x(g - 1)
 
@@ -134,10 +143,12 @@ def tile_routed_moe_kernel(tc, xT, w, offs, out):
                 pieces = w_raw[2 * d + j]
                 span = PASSES // len(pieces)
                 for h, piece in enumerate(pieces):
-                    nc.scalar.copy(
-                        out=duo[:, j, h * span : (h + 1) * span].rearrange("p g (c i) t -> p g c t i", i=4),
-                        in_=piece[:].rearrange("p g (t c i) -> p g c t i", t=4, i=4),
-                    )
+                    dst = duo[:, j, h * span : (h + 1) * span].rearrange("p g (c i) t -> p g c t i", i=4)
+                    src = piece[:].rearrange("p g (t c i) -> p g c t i", t=4, i=4)
+                    if 2 * d + j == E - 1:
+                        nc.vector.tensor_copy(out=dst, in_=src)
+                    else:
+                        nc.scalar.copy(out=dst, in_=src)
 
         sums = last_pool.tile([P, T], F32, name="last", tag="last")
         for d in range(E // 2):

@@ -18,7 +18,7 @@ PASSES = K // (4 * P)
 CHUNKS = 2 * PASSES
 HALF = T // 2
 BANK = 4
-HEAD_CUTS = (4, 2)
+HEAD_CUTS = (4, 2, 2)
 
 
 def tile_routed_moe_kernel(tc, xT, w, offs, out):
@@ -47,7 +47,7 @@ def tile_routed_moe_kernel(tc, xT, w, offs, out):
         x_raw = []
         for i in range(CHUNKS):
             src = x_view[i // 2, i % 2]
-            if i < 2:
+            if i < len(HEAD_CUTS):
                 pieces = []
                 cuts = HEAD_CUTS[i]
                 for h in range(cuts):
@@ -90,10 +90,15 @@ def tile_routed_moe_kernel(tc, xT, w, offs, out):
         def gather_x(i):
             g, u = i // 2, i % 2
             r = CHUNKS - 1 - i
-            if u == 0:
-                planes = slot_pool.tile([P, 2, T], U32, name="planes", align_bytes=64)
-                gathered[g] = planes
-            dst = gathered[g][:, u, :]
+            if g == PASSES - 1:
+                if u == 0:
+                    open_quads(g)
+                dst = grouped[g][:].bitcast(U32).rearrange("p (s u) -> p s u", u=2)[:, :, u]
+            else:
+                if u == 0:
+                    planes = slot_pool.tile([P, 2, T], U32, name="planes", align_bytes=64)
+                    gathered[g] = planes
+                dst = gathered[g][:, u, :]
             if i == 0:
                 for s0 in range(0, T, HALF):
                     nc.vector.tensor_copy(
@@ -113,12 +118,6 @@ def tile_routed_moe_kernel(tc, xT, w, offs, out):
                 in_=gathered[g][:].bitcast(I32).rearrange("p u s -> p s u"),
             )
 
-        def interleave_vector(g):
-            nc.vector.tensor_copy(
-                out=grouped[g][:].bitcast(I32).rearrange("p (s u) -> p s u", u=2),
-                in_=gathered[g][:].bitcast(I32).rearrange("p u s -> p s u"),
-            )
-
         def quantize_x(g):
             nc.vector.quantize_mx(out=x_codes[:, g, :].bitcast(FP8X4), scales=x_scales[:, g, :], in_=grouped[g][:])
 
@@ -127,11 +126,9 @@ def tile_routed_moe_kernel(tc, xT, w, offs, out):
         for g in range(PASSES):
             gather_x(2 * g)
             gather_x(2 * g + 1)
-            open_quads(g)
             if g < PASSES - 1:
+                open_quads(g)
                 interleave_pool(g)
-            else:
-                interleave_vector(g)
             if g >= 1:
                 quantize_x(g - 1)
 

@@ -19,6 +19,7 @@ CHUNKS = 2 * PASSES
 HALF = T // 2
 BANK = 4
 HEAD_CUTS = (4, 2, 2)
+GROUPS = ((0, 1), (1, 4), (4, 8))
 
 
 def tile_routed_moe_kernel(tc, xT, w, offs, out):
@@ -30,7 +31,7 @@ def tile_routed_moe_kernel(tc, xT, w, offs, out):
         last_pool = ctx.enter_context(tc.tile_pool(name="last_pool", bufs=1))
         slot_pool = ctx.enter_context(tc.tile_pool(name="slot_pool", bufs=2))
         weight_pool = ctx.enter_context(tc.tile_pool(name="weight_pool", bufs=E // 2))
-        psum = ctx.enter_context(tc.psum_pool(name="psum", bufs=E // BANK))
+        psum = ctx.enter_context(tc.psum_pool(name="psum", bufs=len(GROUPS)))
 
         offsets = keep.tile([P, T // 16], U16, name="offsets")
         nc.sync.dma_start(offsets[:], offs)
@@ -147,7 +148,13 @@ def tile_routed_moe_kernel(tc, xT, w, offs, out):
                     else:
                         nc.scalar.copy(out=dst, in_=src)
 
+        first_sums = keep.tile([P, C], F32, name="first_sums")
         sums = last_pool.tile([P, T], F32, name="last", tag="last")
+
+        def scatter(values, e0, e1):
+            nc.vector.tensor_copy(out=out_sb[:].indirect(offsets[:, e0 * C // 16 : e1 * C // 16]), in_=values)
+
+        banks = {}
         for d in range(E // 2):
             if d < E // 2 - 1:
                 nc.vector.quantize_mx(
@@ -164,12 +171,15 @@ def tile_routed_moe_kernel(tc, xT, w, offs, out):
                     )
             if d == 0:
                 quantize_x(PASSES - 1)
-            if d % 2 == 0:
-                acc = psum.tile([P, BANK * C], F32, name="acc")
             for e in (2 * d, 2 * d + 1):
+                for e0, e1 in GROUPS:
+                    if e == e0:
+                        acc = psum.tile([P, BANK * C], F32, name="acc")
+                        banks[e0] = acc
+                        first = e0
                 for g in range(PASSES):
                     nc.tensor.matmul_mx(
-                        out=acc[:, (e % BANK) * C : (e % BANK + 1) * C],
+                        out=acc[:, (e - first) * C : (e - first + 1) * C],
                         lhsT=w_codes[:, e, g * N : (g + 1) * N].bitcast(FP8X4),
                         lhsT_scale=w_scales[:, e, g * N : (g + 1) * N],
                         rhs=x_codes[:, g, e * C : (e + 1) * C].bitcast(FP8X4),
@@ -177,12 +187,12 @@ def tile_routed_moe_kernel(tc, xT, w, offs, out):
                         start=(g == 0),
                         stop=(g == PASSES - 1),
                     )
-            if d % 2 == 1:
-                s0 = (d // 2) * BANK * C
-                nc.scalar.copy(out=sums[:, s0 : s0 + BANK * C], in_=acc[:])
-        for s0 in range(0, T, BANK * C):
-            nc.vector.tensor_copy(
-                out=out_sb[:].indirect(offsets[:, s0 // 16 : (s0 + BANK * C) // 16]),
-                in_=sums[:, s0 : s0 + BANK * C],
-            )
+            if d == 1:
+                nc.vector.tensor_copy(out=first_sums[:], in_=banks[0][:, 0:C])
+                scatter(first_sums[:], 0, 1)
+                nc.scalar.copy(out=sums[:, C : 4 * C], in_=banks[1][:, 0 : 3 * C])
+            if d == 3:
+                nc.scalar.copy(out=sums[:, 4 * C : 8 * C], in_=banks[4][:])
+        scatter(sums[:, C : 4 * C], 1, 4)
+        scatter(sums[:, 4 * C : 8 * C], 4, 8)
         nc.sync.dma_start(out, out_sb[:])

@@ -19,7 +19,10 @@ CHUNKS = 2 * PASSES
 HALF = T // 2
 BANK = 4
 HEAD_CUTS = (4, 2, 2)
-GROUPS = ((0, 1), (1, 4), (4, 8))
+SHARED_CASTS = (1, 2)
+MULT = mybir.AluOpType.mult
+ADD = mybir.AluOpType.add
+GROUPS = ((0, 2), (2, 4), (4, 8))
 
 
 def tile_routed_moe_kernel(tc, xT, w, offs, out):
@@ -30,8 +33,9 @@ def tile_routed_moe_kernel(tc, xT, w, offs, out):
         head_pool = ctx.enter_context(tc.tile_pool(name="head_pool", bufs=1))
         last_pool = ctx.enter_context(tc.tile_pool(name="last_pool", bufs=1))
         slot_pool = ctx.enter_context(tc.tile_pool(name="slot_pool", bufs=2))
-        weight_pool = ctx.enter_context(tc.tile_pool(name="weight_pool", bufs=E // 2))
+        weight_pool = ctx.enter_context(tc.tile_pool(name="weight_pool", bufs=E // 2 - 1))
         psum = ctx.enter_context(tc.psum_pool(name="psum", bufs=len(GROUPS)))
+        relay = ctx.enter_context(tc.tile_pool(name="relay", bufs=1))
 
         offsets = keep.tile([P, T // 16], U16, name="offsets")
         nc.sync.dma_start(offsets[:], offs)
@@ -82,6 +86,16 @@ def tile_routed_moe_kernel(tc, xT, w, offs, out):
                 src = piece[:].rearrange("p e n -> p n e")
                 if i == 0:
                     nc.vector.tensor_copy(out=dst, in_=src)
+                elif i in SHARED_CASTS and h == len(x_raw[i]) - 1:
+                    nc.scalar.copy(out=dst[:, 0 : width // 2, :], in_=src[:, 0 : width // 2, :])
+                    nc.gpsimd.tensor_scalar(
+                        out=dst[:, width // 2 : width, :],
+                        in0=src[:, width // 2 : width, :],
+                        scalar1=1.0,
+                        scalar2=0.0,
+                        op0=MULT,
+                        op1=ADD,
+                    )
                 else:
                     nc.scalar.copy(out=dst, in_=src)
 
@@ -135,7 +149,10 @@ def tile_routed_moe_kernel(tc, xT, w, offs, out):
 
         w_grouped = []
         for d in range(E // 2):
-            duo = weight_pool.tile([P, 2, PASSES, N, 4], BF16, name="duo", align_bytes=64)
+            if d == 1:
+                duo = relay.tile([P, 2, PASSES, N, 4], BF16, name="relay_duo", tag="relay", align_bytes=64)
+            else:
+                duo = weight_pool.tile([P, 2, PASSES, N, 4], BF16, name="duo", align_bytes=64)
             w_grouped.append(duo)
             for j in range(2):
                 pieces = w_raw[2 * d + j]
@@ -148,7 +165,6 @@ def tile_routed_moe_kernel(tc, xT, w, offs, out):
                     else:
                         nc.scalar.copy(out=dst, in_=src)
 
-        first_sums = keep.tile([P, C], F32, name="first_sums")
         sums = last_pool.tile([P, T], F32, name="last", tag="last")
 
         def scatter(values, e0, e1):
@@ -188,11 +204,12 @@ def tile_routed_moe_kernel(tc, xT, w, offs, out):
                         stop=(g == PASSES - 1),
                     )
             if d == 1:
-                nc.vector.tensor_copy(out=first_sums[:], in_=banks[0][:, 0:C])
-                scatter(first_sums[:], 0, 1)
-                nc.scalar.copy(out=sums[:, C : 4 * C], in_=banks[1][:, 0 : 3 * C])
+                first_sums = relay.tile([P, 2 * C], F32, name="first_sums", tag="relay", align_bytes=64)
+                nc.vector.tensor_copy(out=first_sums[:], in_=banks[0][:, 0 : 2 * C])
+                scatter(first_sums[:], 0, 2)
+                nc.scalar.copy(out=sums[:, 2 * C : 4 * C], in_=banks[2][:, 0 : 2 * C])
             if d == 3:
                 nc.scalar.copy(out=sums[:, 4 * C : 8 * C], in_=banks[4][:])
-        scatter(sums[:, C : 4 * C], 1, 4)
+        scatter(sums[:, 2 * C : 4 * C], 2, 4)
         scatter(sums[:, 4 * C : 8 * C], 4, 8)
         nc.sync.dma_start(out, out_sb[:])

@@ -17,12 +17,12 @@ P = 128
 PASSES = K // (4 * P)
 CHUNKS = 2 * PASSES
 HALF = T // 2
-BANK = 4
 HEAD_CUTS = (4, 2, 2)
 SHARED_CASTS = (1, 2)
 MULT = mybir.AluOpType.mult
 ADD = mybir.AluOpType.add
-GROUPS = ((0, 2), (2, 4), (4, 8))
+GROUPS = ((0, 2), (2, 4), (4, 6), (6, 8))
+BANK = 2
 
 
 def tile_routed_moe_kernel(tc, xT, w, offs, out):
@@ -33,7 +33,7 @@ def tile_routed_moe_kernel(tc, xT, w, offs, out):
         head_pool = ctx.enter_context(tc.tile_pool(name="head_pool", bufs=1))
         last_pool = ctx.enter_context(tc.tile_pool(name="last_pool", bufs=1))
         slot_pool = ctx.enter_context(tc.tile_pool(name="slot_pool", bufs=2))
-        weight_pool = ctx.enter_context(tc.tile_pool(name="weight_pool", bufs=E // 2 - 1))
+        weight_pool = ctx.enter_context(tc.tile_pool(name="weight_pool", bufs=2))
         psum = ctx.enter_context(tc.psum_pool(name="psum", bufs=len(GROUPS)))
         relay = ctx.enter_context(tc.tile_pool(name="relay", bufs=1))
 
@@ -150,7 +150,9 @@ def tile_routed_moe_kernel(tc, xT, w, offs, out):
         w_grouped = []
         for d in range(E // 2):
             if d == 1:
-                duo = relay.tile([P, 2, PASSES, N, 4], BF16, name="relay_duo", tag="relay", align_bytes=64)
+                duo = relay.tile([P, 2, PASSES, N, 4], BF16, name="relay_duo", tag="relay1", align_bytes=64)
+            elif d == 2:
+                duo = relay.tile([P, 2, PASSES, N, 4], BF16, name="relay_duo2", tag="relay2", align_bytes=64)
             else:
                 duo = weight_pool.tile([P, 2, PASSES, N, 4], BF16, name="duo", align_bytes=64)
             w_grouped.append(duo)
@@ -165,7 +167,7 @@ def tile_routed_moe_kernel(tc, xT, w, offs, out):
                     else:
                         nc.scalar.copy(out=dst, in_=src)
 
-        sums = last_pool.tile([P, T], F32, name="last", tag="last")
+        sums = last_pool.tile([P, 4 * C], F32, name="last", tag="last")
 
         def scatter(values, e0, e1):
             nc.vector.tensor_copy(out=out_sb[:].indirect(offsets[:, e0 * C // 16 : e1 * C // 16]), in_=values)
@@ -203,13 +205,13 @@ def tile_routed_moe_kernel(tc, xT, w, offs, out):
                         start=(g == 0),
                         stop=(g == PASSES - 1),
                     )
-            if d == 1:
-                first_sums = relay.tile([P, 2 * C], F32, name="first_sums", tag="relay", align_bytes=64)
-                nc.vector.tensor_copy(out=first_sums[:], in_=banks[0][:, 0 : 2 * C])
-                scatter(first_sums[:], 0, 2)
-                nc.scalar.copy(out=sums[:, 2 * C : 4 * C], in_=banks[2][:, 0 : 2 * C])
+            if d in (1, 2):
+                early = relay.tile([P, 2 * C], F32, name="early_sums", tag="relay%d" % d, align_bytes=64)
+                nc.vector.tensor_copy(out=early[:], in_=banks[2 * d - 2][:])
+                scatter(early[:], 2 * d - 2, 2 * d)
             if d == 3:
-                nc.scalar.copy(out=sums[:, 4 * C : 8 * C], in_=banks[4][:])
-        scatter(sums[:, 2 * C : 4 * C], 2, 4)
-        scatter(sums[:, 4 * C : 8 * C], 4, 8)
+                for e0 in (4, 6):
+                    nc.scalar.copy(out=sums[:, (e0 - 4) * C : (e0 - 2) * C], in_=banks[e0][:])
+        for e0 in (4, 6):
+            scatter(sums[:, (e0 - 4) * C : (e0 - 2) * C], e0, e0 + 2)
         nc.sync.dma_start(out, out_sb[:])

@@ -19,6 +19,7 @@ CHUNKS = 2 * PASSES
 HALF = T // 2
 HEAD_CUTS = (4, 2, 2)
 SHARED_CASTS = (1, 2)
+HELD = 5
 MULT = mybir.AluOpType.mult
 ADD = mybir.AluOpType.add
 GROUPS = ((0, 2), (2, 4), (4, 6), (6, 8))
@@ -29,13 +30,13 @@ def tile_routed_moe_kernel(tc, xT, w, offs, out):
     nc = tc.nc
     with ExitStack() as ctx:
         keep = ctx.enter_context(tc.tile_pool(name="keep", bufs=1))
-        raw_pool = ctx.enter_context(tc.tile_pool(name="raw_pool", bufs=7))
+        raw_pool = ctx.enter_context(tc.tile_pool(name="raw_pool", bufs=6))
         head_pool = ctx.enter_context(tc.tile_pool(name="head_pool", bufs=1))
         last_pool = ctx.enter_context(tc.tile_pool(name="last_pool", bufs=1))
         slot_pool = ctx.enter_context(tc.tile_pool(name="slot_pool", bufs=2))
-        weight_pool = ctx.enter_context(tc.tile_pool(name="weight_pool", bufs=2))
+        weight_pool = ctx.enter_context(tc.tile_pool(name="weight_pool", bufs=E // 2 - 1))
         psum = ctx.enter_context(tc.psum_pool(name="psum", bufs=len(GROUPS)))
-        relay = ctx.enter_context(tc.tile_pool(name="relay", bufs=1))
+        hold_pool = ctx.enter_context(tc.tile_pool(name="hold_pool", bufs=1))
 
         offsets = keep.tile([P, T // 16], U16, name="offsets")
         nc.sync.dma_start(offsets[:], offs)
@@ -68,7 +69,10 @@ def tile_routed_moe_kernel(tc, xT, w, offs, out):
         for e in range(E):
             src = w[e].rearrange("(g p t) n -> p g (t n)", p=P, t=4)
             if e < E - 1:
-                raw = raw_pool.tile([P, PASSES, 4 * N], F32, name="raw", tag="raw")
+                if e == HELD:
+                    raw = hold_pool.tile([P, PASSES, 4 * N], F32, name="held", tag="held", align_bytes=64)
+                else:
+                    raw = raw_pool.tile([P, PASSES, 4 * N], F32, name="raw", tag="raw")
                 nc.sync.dma_start(raw[:], src)
                 w_raw.append([raw])
             else:
@@ -150,9 +154,7 @@ def tile_routed_moe_kernel(tc, xT, w, offs, out):
         w_grouped = []
         for d in range(E // 2):
             if d == 1:
-                duo = relay.tile([P, 2, PASSES, N, 4], BF16, name="relay_duo", tag="relay1", align_bytes=64)
-            elif d == 2:
-                duo = relay.tile([P, 2, PASSES, N, 4], BF16, name="relay_duo2", tag="relay2", align_bytes=64)
+                duo = hold_pool.tile([P, 2, PASSES, N, 4], BF16, name="relay_duo", tag="relay", align_bytes=64)
             else:
                 duo = weight_pool.tile([P, 2, PASSES, N, 4], BF16, name="duo", align_bytes=64)
             w_grouped.append(duo)
@@ -162,8 +164,15 @@ def tile_routed_moe_kernel(tc, xT, w, offs, out):
                 for h, piece in enumerate(pieces):
                     dst = duo[:, j, h * span : (h + 1) * span].rearrange("p g (c i) t -> p g c t i", i=4)
                     src = piece[:].rearrange("p g (t c i) -> p g c t i", t=4, i=4)
-                    if 2 * d + j == E - 1:
-                        nc.vector.tensor_copy(out=dst, in_=src)
+                    if 2 * d + j == E - 1 and h == 0:
+                        nc.gpsimd.tensor_scalar(
+                            out=duo[:, j, 0:span],
+                            in0=piece[:].rearrange("p g (t n) -> p g n t", t=4),
+                            scalar1=1.0,
+                            scalar2=0.0,
+                            op0=MULT,
+                            op1=ADD,
+                        )
                     else:
                         nc.scalar.copy(out=dst, in_=src)
 
@@ -206,8 +215,11 @@ def tile_routed_moe_kernel(tc, xT, w, offs, out):
                         stop=(g == PASSES - 1),
                     )
             if d in (1, 2):
-                early = relay.tile([P, 2 * C], F32, name="early_sums", tag="relay%d" % d, align_bytes=64)
-                nc.vector.tensor_copy(out=early[:], in_=banks[2 * d - 2][:])
+                early = hold_pool.tile([P, 2 * C], F32, name="early%d" % d, tag="relay" if d == 1 else "held", align_bytes=64)
+                if d == 1:
+                    nc.vector.tensor_copy(out=early[:], in_=banks[0][:])
+                else:
+                    nc.scalar.copy(out=early[:], in_=banks[2][:])
                 scatter(early[:], 2 * d - 2, 2 * d)
             if d == 3:
                 for e0 in (4, 6):

@@ -17,12 +17,12 @@ P = 128
 PASSES = K // (4 * P)
 CHUNKS = 2 * PASSES
 HALF = T // 2
-HEAD_CUTS = (4, 2, 2)
+HEAD_CUTS = (2, 1, 1)
 SHARED_CASTS = (1, 2)
 HELD = 5
 MULT = mybir.AluOpType.mult
 ADD = mybir.AluOpType.add
-GROUPS = ((0, 2), (2, 4), (4, 6), (6, 8))
+GROUPS = ((0, 1), (1, 2), (2, 4), (4, 6), (6, 8))
 BANK = 2
 
 
@@ -34,17 +34,16 @@ def tile_routed_moe_kernel(tc, xT, w, offs, out):
         head_pool = ctx.enter_context(tc.tile_pool(name="head_pool", bufs=1))
         last_pool = ctx.enter_context(tc.tile_pool(name="last_pool", bufs=1))
         slot_pool = ctx.enter_context(tc.tile_pool(name="slot_pool", bufs=2))
-        weight_pool = ctx.enter_context(tc.tile_pool(name="weight_pool", bufs=E // 2 - 1))
+        weight_pool = ctx.enter_context(tc.tile_pool(name="weight_pool", bufs=E // 2 - 2))
         psum = ctx.enter_context(tc.psum_pool(name="psum", bufs=len(GROUPS)))
         hold_pool = ctx.enter_context(tc.tile_pool(name="hold_pool", bufs=1))
 
         offsets = keep.tile([P, T // 16], U16, name="offsets")
-        nc.sync.dma_start(offsets[:], offs)
 
         pairs = keep.tile([P, CHUNKS, T, 2], BF16, name="pairs", align_bytes=64)
         pair_words = pairs[:].rearrange("p r n e -> p (r n e)").bitcast(U32)
-        x_codes = keep.tile([P, PASSES, T], U32, name="x_codes", align_bytes=64)
-        x_scales = keep.tile([P, PASSES, T], U8, name="x_scales", align_bytes=64)
+        x_codes = []
+        x_scales = []
         w_codes = keep.tile([P, E, PASSES * N], U32, name="w_codes", align_bytes=64)
         w_scales = keep.tile([P, E, PASSES * N], U8, name="w_scales", align_bytes=64)
         out_sb = keep.tile([P, T], F32, name="out_sb")
@@ -60,6 +59,8 @@ def tile_routed_moe_kernel(tc, xT, w, offs, out):
                     part = head_pool.tile([P, 2, T // cuts], F32, name="part%d_%d" % (i, h))
                     nc.sync.dma_start(part[:], src[:, :, h * (T // cuts) : (h + 1) * (T // cuts)])
                     pieces.append(part)
+                if i == 0:
+                    nc.sync.dma_start(offsets[:], offs)
             else:
                 raw = raw_pool.tile([P, 2, T], F32, name="raw", tag="raw")
                 nc.sync.dma_start(raw[:], src)
@@ -138,7 +139,11 @@ def tile_routed_moe_kernel(tc, xT, w, offs, out):
             )
 
         def quantize_x(g):
-            nc.vector.quantize_mx(out=x_codes[:, g, :].bitcast(FP8X4), scales=x_scales[:, g, :], in_=grouped[g][:])
+            pool, tag = (hold_pool, "first") if g == PASSES - 1 else (keep, "both%d" % g)
+            both = pool.tile([P, T * 5], U8, name="both%d" % g, tag=tag, align_bytes=64)
+            x_codes.append(both[:, 0 : T * 4].bitcast(U32))
+            x_scales.append(both[:, T * 4 : T * 5])
+            nc.vector.quantize_mx(out=x_codes[g].bitcast(FP8X4), scales=x_scales[g], in_=grouped[g][:])
 
         for i in range(CHUNKS):
             cast_x(i)
@@ -153,7 +158,9 @@ def tile_routed_moe_kernel(tc, xT, w, offs, out):
 
         w_grouped = []
         for d in range(E // 2):
-            if d == 1:
+            if d == 0:
+                duo = hold_pool.tile([P, 2, PASSES, N, 4], BF16, name="first_duo", tag="first", align_bytes=64)
+            elif d == 1:
                 duo = hold_pool.tile([P, 2, PASSES, N, 4], BF16, name="relay_duo", tag="relay", align_bytes=64)
             else:
                 duo = weight_pool.tile([P, 2, PASSES, N, 4], BF16, name="duo", align_bytes=64)
@@ -182,6 +189,19 @@ def tile_routed_moe_kernel(tc, xT, w, offs, out):
             nc.vector.tensor_copy(out=out_sb[:].indirect(offsets[:, e0 * C // 16 : e1 * C // 16]), in_=values)
 
         banks = {}
+
+        def multiply(e, first, g0, g1):
+            for g in range(g0, g1):
+                nc.tensor.matmul_mx(
+                    out=banks[first][:, (e - first) * C : (e - first + 1) * C],
+                    lhsT=w_codes[:, e, g * N : (g + 1) * N].bitcast(FP8X4),
+                    lhsT_scale=w_scales[:, e, g * N : (g + 1) * N],
+                    rhs=x_codes[g][:, e * C : (e + 1) * C].bitcast(FP8X4),
+                    rhs_scale=x_scales[g][:, e * C : (e + 1) * C],
+                    start=(g == 0),
+                    stop=(g == PASSES - 1),
+                )
+
         for d in range(E // 2):
             if d < E // 2 - 1:
                 nc.vector.quantize_mx(
@@ -196,28 +216,22 @@ def tile_routed_moe_kernel(tc, xT, w, offs, out):
                         scales=w_scales[:, 2 * d + j, :],
                         in_=w_grouped[d][:, j].rearrange("p g n t -> p (g n t)"),
                     )
-            if d == 0:
-                quantize_x(PASSES - 1)
             for e in (2 * d, 2 * d + 1):
                 for e0, e1 in GROUPS:
                     if e == e0:
                         acc = psum.tile([P, BANK * C], F32, name="acc")
                         banks[e0] = acc
                         first = e0
-                for g in range(PASSES):
-                    nc.tensor.matmul_mx(
-                        out=acc[:, (e - first) * C : (e - first + 1) * C],
-                        lhsT=w_codes[:, e, g * N : (g + 1) * N].bitcast(FP8X4),
-                        lhsT_scale=w_scales[:, e, g * N : (g + 1) * N],
-                        rhs=x_codes[:, g, e * C : (e + 1) * C].bitcast(FP8X4),
-                        rhs_scale=x_scales[:, g, e * C : (e + 1) * C],
-                        start=(g == 0),
-                        stop=(g == PASSES - 1),
-                    )
+                multiply(e, first, 0, PASSES - 1 if d == 0 else PASSES)
+            if d == 0:
+                quantize_x(PASSES - 1)
+                for e in range(2):
+                    multiply(e, e, PASSES - 1, PASSES)
             if d in (1, 2):
                 early = hold_pool.tile([P, 2 * C], F32, name="early%d" % d, tag="relay" if d == 1 else "held", align_bytes=64)
                 if d == 1:
-                    nc.vector.tensor_copy(out=early[:], in_=banks[0][:])
+                    for e in range(2):
+                        nc.vector.tensor_copy(out=early[:, e * C : (e + 1) * C], in_=banks[e][:, 0:C])
                 else:
                     nc.scalar.copy(out=early[:], in_=banks[2][:])
                 scatter(early[:], 2 * d - 2, 2 * d)

from contextlib import ExitStack

import concourse.mybir as mybir

K, T, E, C, N = 2048, 1024, 8, 128, 128
FLOPS = 2 * K * N * E * C

F32 = mybir.dt.float32
BF16 = mybir.dt.bfloat16
U32 = mybir.dt.uint32
I32 = mybir.dt.int32
U16 = mybir.dt.uint16
U8 = mybir.dt.uint8
FP8X4 = mybir.dt.float8_e4m3fn_x4

P = 128
PASSES = K // (4 * P)
CHUNKS = 2 * PASSES
HALF = T // 2
HEAD_CUTS = (2, 1, 1)
SHARED_CASTS = (1, 2)
HELD = 5
MULT = mybir.AluOpType.mult
ADD = mybir.AluOpType.add
GROUPS = ((0, 1), (1, 2), (2, 4), (4, 6), (6, 8))
BANK = 2


def tile_routed_moe_kernel(tc, xT, w, offs, out):
    nc = tc.nc
    with ExitStack() as ctx:
        keep = ctx.enter_context(tc.tile_pool(name="keep", bufs=1))
        raw_pool = ctx.enter_context(tc.tile_pool(name="raw_pool", bufs=6))
        head_pool = ctx.enter_context(tc.tile_pool(name="head_pool", bufs=1))
        last_pool = ctx.enter_context(tc.tile_pool(name="last_pool", bufs=1))
        slot_pool = ctx.enter_context(tc.tile_pool(name="slot_pool", bufs=2))
        weight_pool = ctx.enter_context(tc.tile_pool(name="weight_pool", bufs=E // 2 - 2))
        psum = ctx.enter_context(tc.psum_pool(name="psum", bufs=len(GROUPS)))
        hold_pool = ctx.enter_context(tc.tile_pool(name="hold_pool", bufs=1))

        offsets = keep.tile([P, T // 16], U16, name="offsets")

        pairs = keep.tile([P, CHUNKS, T, 2], BF16, name="pairs", align_bytes=64)
        pair_words = pairs[:].rearrange("p r n e -> p (r n e)").bitcast(U32)
        x_codes = []
        x_scales = []
        w_codes = keep.tile([P, E, PASSES * N], U32, name="w_codes", align_bytes=64)
        w_scales = keep.tile([P, E, PASSES * N], U8, name="w_scales", align_bytes=64)
        out_sb = keep.tile([P, T], F32, name="out_sb")

        x_view = xT.rearrange("(g p u e) n -> g u p e n", g=PASSES, p=P, u=2, e=2)
        x_raw = []
        for i in range(CHUNKS):
            src = x_view[i // 2, i % 2]
            if i < len(HEAD_CUTS):
                pieces = []
                cuts = HEAD_CUTS[i]
                for h in range(cuts):
                    part = head_pool.tile([P, 2, T // cuts], F32, name="part%d_%d" % (i, h))
                    nc.sync.dma_start(part[:], src[:, :, h * (T // cuts) : (h + 1) * (T // cuts)])
                    pieces.append(part)
                if i == 0:
                    nc.sync.dma_start(offsets[:], offs)
            else:
                raw = raw_pool.tile([P, 2, T], F32, name="raw", tag="raw")
                nc.sync.dma_start(raw[:], src)
                pieces = [raw]
            x_raw.append(pieces)
        w_raw = []
        for e in range(E):
            src = w[e].rearrange("(g p t) n -> p g (t n)", p=P, t=4)
            if e < E - 1:
                if e == HELD:
                    raw = hold_pool.tile([P, PASSES, 4 * N], F32, name="held", tag="held", align_bytes=64)
                else:
                    raw = raw_pool.tile([P, PASSES, 4 * N], F32, name="raw", tag="raw")
                nc.sync.dma_start(raw[:], src)
                w_raw.append([raw])
            else:
                early = head_pool.tile([P, PASSES // 2, 4 * N], F32, name="early")
                nc.sync.dma_start(early[:], src[:, 0 : PASSES // 2, :])
                late = last_pool.tile([P, PASSES // 2, 4 * N], F32, name="last", tag="last")
                nc.sync.dma_start(late[:], src[:, PASSES // 2 : PASSES, :])
                w_raw.append([early, late])

        def cast_x(i):
            region = pairs[:, CHUNKS - 1 - i]
            width = T // len(x_raw[i])
            for h, piece in enumerate(x_raw[i]):
                dst = region[:, h * width : (h + 1) * width, :]
                src = piece[:].rearrange("p e n -> p n e")
                if i == 0:
                    nc.vector.tensor_copy(out=dst, in_=src)
                elif i in SHARED_CASTS and h == len(x_raw[i]) - 1:
                    nc.scalar.copy(out=dst[:, 0 : width // 2, :], in_=src[:, 0 : width // 2, :])
                    nc.gpsimd.tensor_scalar(
                        out=dst[:, width // 2 : width, :],
                        in0=src[:, width // 2 : width, :],
                        scalar1=1.0,
                        scalar2=0.0,
                        op0=MULT,
                        op1=ADD,
                    )
                else:
                    nc.scalar.copy(out=dst, in_=src)

        gathered = {}
        grouped = {}

        def gather_x(i):
            g, u = i // 2, i % 2
            r = CHUNKS - 1 - i
            if g == PASSES - 1:
                if u == 0:
                    open_quads(g)
                dst = grouped[g][:].bitcast(U32).rearrange("p (s u) -> p s u", u=2)[:, :, u]
            else:
                if u == 0:
                    planes = slot_pool.tile([P, 2, T], U32, name="planes", align_bytes=64)
                    gathered[g] = planes
                dst = gathered[g][:, u, :]
            if i == 0:
                for s0 in range(0, T, HALF):
                    nc.vector.tensor_copy(
                        out=dst[:, s0 : s0 + HALF],
                        in_=pair_words[:, r * T : (r + 1) * T].indirect(offsets[:, s0 // 16 : (s0 + HALF) // 16]),
                    )
            else:
                nc.vector.tensor_copy(out=dst, in_=pair_words[:, r * T : (r + 2) * T].indirect(offsets[:]))

        def open_quads(g):
            quads = slot_pool.tile([P, T * 4], BF16, name="quads", align_bytes=64)
            grouped[g] = quads

        def interleave_pool(g):
            nc.gpsimd.tensor_copy(
                out=grouped[g][:].bitcast(I32).rearrange("p (s u) -> p s u", u=2),
                in_=gathered[g][:].bitcast(I32).rearrange("p u s -> p s u"),
            )

        def quantize_x(g):
            pool, tag = (hold_pool, "first") if g == PASSES - 1 else (keep, "both%d" % g)
            both = pool.tile([P, T * 5], U8, name="both%d" % g, tag=tag, align_bytes=64)
            x_codes.append(both[:, 0 : T * 4].bitcast(U32))
            x_scales.append(both[:, T * 4 : T * 5])
            nc.vector.quantize_mx(out=x_codes[g].bitcast(FP8X4), scales=x_scales[g], in_=grouped[g][:])

        for i in range(CHUNKS):
            cast_x(i)
        for g in range(PASSES):
            gather_x(2 * g)
            gather_x(2 * g + 1)
            if g < PASSES - 1:
                open_quads(g)
                interleave_pool(g)
            if g >= 1:
                quantize_x(g - 1)

        w_grouped = []
        for d in range(E // 2):
            if d == 0:
                duo = hold_pool.tile([P, 2, PASSES, N, 4], BF16, name="first_duo", tag="first", align_bytes=64)
            elif d == 1:
                duo = hold_pool.tile([P, 2, PASSES, N, 4], BF16, name="relay_duo", tag="relay", align_bytes=64)
            else:
                duo = weight_pool.tile([P, 2, PASSES, N, 4], BF16, name="duo", align_bytes=64)
            w_grouped.append(duo)
            for j in range(2):
                pieces = w_raw[2 * d + j]
                span = PASSES // len(pieces)
                for h, piece in enumerate(pieces):
                    dst = duo[:, j, h * span : (h + 1) * span].rearrange("p g (c i) t -> p g c t i", i=4)
                    src = piece[:].rearrange("p g (t c i) -> p g c t i", t=4, i=4)
                    if 2 * d + j == E - 1 and h == 0:
                        nc.gpsimd.tensor_scalar(
                            out=duo[:, j, 0:span],
                            in0=piece[:].rearrange("p g (t n) -> p g n t", t=4),
                            scalar1=1.0,
                            scalar2=0.0,
                            op0=MULT,
                            op1=ADD,
                        )
                    else:
                        nc.scalar.copy(out=dst, in_=src)

        sums = last_pool.tile([P, 4 * C], F32, name="last", tag="last")

        def scatter(values, e0, e1):
            nc.vector.tensor_copy(out=out_sb[:].indirect(offsets[:, e0 * C // 16 : e1 * C // 16]), in_=values)

        banks = {}

        def multiply(e, first, g0, g1):
            for g in range(g0, g1):
                nc.tensor.matmul_mx(
                    out=banks[first][:, (e - first) * C : (e - first + 1) * C],
                    lhsT=w_codes[:, e, g * N : (g + 1) * N].bitcast(FP8X4),
                    lhsT_scale=w_scales[:, e, g * N : (g + 1) * N],
                    rhs=x_codes[g][:, e * C : (e + 1) * C].bitcast(FP8X4),
                    rhs_scale=x_scales[g][:, e * C : (e + 1) * C],
                    start=(g == 0),
                    stop=(g == PASSES - 1),
                )

        for d in range(E // 2):
            if d < E // 2 - 1:
                nc.vector.quantize_mx(
                    out=w_codes[:, 2 * d : 2 * d + 2, :].rearrange("p e c -> p (e c)").bitcast(FP8X4),
                    scales=w_scales[:, 2 * d : 2 * d + 2, :].rearrange("p e c -> p (e c)"),
                    in_=w_grouped[d][:].rearrange("p j g n t -> p (j g n t)"),
                )
            else:
                for j in range(2):
                    nc.vector.quantize_mx(
                        out=w_codes[:, 2 * d + j, :].bitcast(FP8X4),
                        scales=w_scales[:, 2 * d + j, :],
                        in_=w_grouped[d][:, j].rearrange("p g n t -> p (g n t)"),
                    )
            for e in (2 * d, 2 * d + 1):
                for e0, e1 in GROUPS:
                    if e == e0:
                        acc = psum.tile([P, BANK * C], F32, name="acc")
                        banks[e0] = acc
                        first = e0
                multiply(e, first, 0, PASSES - 1 if d == 0 else PASSES)
            if d == 0:
                quantize_x(PASSES - 1)
                for e in range(2):
                    multiply(e, e, PASSES - 1, PASSES)
            if d in (1, 2):
                early = hold_pool.tile([P, 2 * C], F32, name="early%d" % d, tag="relay" if d == 1 else "held", align_bytes=64)
                if d == 1:
                    for e in range(2):
                        nc.vector.tensor_copy(out=early[:, e * C : (e + 1) * C], in_=banks[e][:, 0:C])
                else:
                    nc.scalar.copy(out=early[:], in_=banks[2][:])
                scatter(early[:], 2 * d - 2, 2 * d)
            if d == 3:
                for e0 in (4, 6):
                    nc.scalar.copy(out=sums[:, (e0 - 4) * C : (e0 - 2) * C], in_=banks[e0][:])
        for e0 in (4, 6):
            scatter(sums[:, (e0 - 4) * C : (e0 - 2) * C], e0, e0 + 2)
        nc.sync.dma_start(out, out_sb[:])
